import numpy as np
import ml_dtypes


def mxq(x, axis, fmt="e4m3"):
    dtype, down = {"e4m3": (ml_dtypes.float8_e4m3fn, 7), "e5m2": (ml_dtypes.float8_e5m2, 14)}[fmt]
    v = np.moveaxis(np.asarray(x, np.float32).astype(ml_dtypes.bfloat16).astype(np.float64), axis, -1)
    blocks = v.reshape(v.shape[:-1] + (-1, 32))
    amax = np.abs(blocks).max(-1, keepdims=True)
    byte = np.maximum(np.where(amax > 0, np.frexp(amax)[1] - 1 + 127, 0) - down, 1)
    scale = np.exp2(byte - 127.0)
    codes = (blocks / scale).astype(np.float32).astype(dtype).astype(np.float64)
    return np.moveaxis((codes * scale).reshape(v.shape), -1, axis)


WIDE = False


def mx_kscale(k):
    if not WIDE:
        return np.ones(k)
    levels = np.array([10, -10, 5, -5, 0])
    if k % 512:
        return np.exp2(np.random.permutation(np.resize(levels, k // 32))).repeat(32)
    a = np.empty((k // 512, 16))
    for p in range(k // 512):
        a[p, :8] = np.random.permutation(np.resize(levels, 8))
        for g in range(8):
            far = levels[np.abs(levels - a[p, g]) >= 10]
            a[p, g + 8] = far[np.random.randint(len(far))]
    return np.exp2(a.ravel()).repeat(32)


BF16 = ml_dtypes.bfloat16


def bf(x):
    return np.asarray(x, np.float32).astype(BF16)


def f64(x):
    return np.asarray(x).astype(np.float64)


E2M1 = np.array([0.0, 0.5, 1.0, 1.5, 2.0, 3.0, 4.0, 6.0, -0.0, -0.5, -1.0, -1.5, -2.0, -3.0, -4.0, -6.0])


def pack_weight(w, fmt):
    k, n = w.shape
    w = f64(bf(w)).reshape(k // 32, 32, n)
    amax = np.abs(w).max(1)
    if fmt == "e4m3":
        byte = np.frexp(amax)[1] - 1 + 127 - 7
    else:
        mant, ex = np.frexp(amax / 6.0)
        byte = np.where(mant > 0.5, ex, ex - 1) + 127
    byte = np.clip(np.where(amax > 0, byte, 1), 1, 254)
    scaled = (w * np.exp2(127.0 - byte)[:, None, :]).reshape(k, n).astype(np.float32)
    by_word = np.ascontiguousarray(scaled.reshape(k // 512, 128, 4, n).transpose(0, 1, 3, 2))
    if fmt == "e4m3":
        words = by_word.astype(ml_dtypes.float8_e4m3fn).view(np.uint8)
    else:
        c = by_word.astype(ml_dtypes.float4_e2m1fn).view(np.uint8) & 0xF
        words = c[..., 0::2] | (c[..., 1::2] << 4)
    return np.ascontiguousarray(words), np.ascontiguousarray(byte.astype(np.uint8).reshape(k // 512, 16, n))


def unpack_weight(words, scales, fmt):
    g, p, n, _ = words.shape
    if fmt == "e4m3":
        vals = np.ascontiguousarray(words).view(ml_dtypes.float8_e4m3fn).astype(np.float64)
    else:
        nib = np.empty((g, p, n, 4), np.uint8)
        nib[..., 0::2] = words & 0xF
        nib[..., 1::2] = words >> 4
        vals = E2M1[nib]
    vals = vals * np.repeat(np.exp2(scales.astype(np.float64) - 127.0), 8, axis=1)[..., None]
    return vals.transpose(0, 1, 3, 2).reshape(g * 512, n)
def pack4(w):
    words, scales = pack_weight(w, "e2m1")
    return words.reshape(words.shape[0], 128, -1), scales


def unpack4(words, scales):
    return unpack_weight(words.reshape(words.shape[0], 128, -1, 2), scales, "e2m1")


S, P, D, F = 256, 8, 2048, 1024

EPS = 0.1


def rms_norm(x, gain):
    return x / np.sqrt(np.mean(x * x, axis=-1, keepdims=True) + EPS) * gain


def draw0():
    r, t = mx_kscale(D), mx_kscale(F)
    halves = np.concatenate([np.ones(F), t])
    film = 0.6 * np.random.standard_normal((D, 2 * F)) / np.sqrt(D) / r[:, None] * halves
    film_words, film_scales = pack4(film)
    proj = np.random.standard_normal((F, F)) / np.sqrt(F) / t[:, None]
    proj_words, proj_scales = pack_weight(proj, "e4m3")
    level = np.random.uniform(0.5, 2.0, (S, P, 1))
    return {"cond": bf(np.random.standard_normal((S, D)) * r),
            "film_words": film_words,
            "film_scales": film_scales,
            "film_bias": bf(0.3 * np.random.standard_normal(2 * F) * halves),
            "x": bf(np.random.standard_normal((S, P, F)) * level),
            "gain": bf((1 + 0.1 * np.random.standard_normal(F)) * t),
            "proj_words": proj_words,
            "proj_scales": proj_scales,
            "proj_bias": bf(0.3 * np.random.standard_normal(F))}


def core(cond, film_words, film_scales, film_bias, x, gain, proj_words, proj_scales, proj_bias):
    film = (mxq(f64(cond), 1, "e4m3") @ unpack4(film_words, film_scales)) + f64(film_bias)
    scale = 1 + film[:, :F]
    shift = film[:, F:]
    v = rms_norm(f64(x), f64(gain))
    h = np.maximum(v * scale[:, None, :] + shift[:, None, :], 0)
    h = h.reshape(S * P, F)
    y = mxq(h, 1, "e4m3") @ unpack_weight(proj_words, proj_scales, "e4m3")
    return f64(x) + y.reshape(S, P, F) + f64(proj_bias)


def e4m3fn_bytes(y):
    return np.clip(np.asarray(y, np.float64), -448.0, 448.0).astype(np.float32).astype(ml_dtypes.float8_e4m3fn).view(np.uint8)


def e4m3fn_values(b):
    return np.asarray(b, np.uint8).view(ml_dtypes.float8_e4m3fn).astype(np.float64)


def setup_inputs():
    d = draw0()
    x0 = np.asarray(d['cond']).astype(np.float64)
    s = (np.max(np.abs(x0), axis=(0,), keepdims=True) / 448.0).astype(np.float32)
    out = {}
    for k, v in d.items():
        if k == 'cond':
            out['cond_bytes'] = e4m3fn_bytes(x0 / s.astype(np.float64))
            out['cond_scale'] = s
        else:
            out[k] = v
    return out


def reference(cond_bytes, cond_scale, film_words, film_scales, film_bias, x, gain, proj_words, proj_scales, proj_bias):
    return core(e4m3fn_values(cond_bytes) * cond_scale.astype(np.float64), film_words, film_scales, film_bias, x, gain, proj_words, proj_scales, proj_bias)

@@ -1,0 +1,324 @@
+from contextlib import ExitStack
+
+import concourse.mybir as mybir
+from concourse.masks import make_identity
+
+S, P, D, F = 256, 8, 2048, 1024
+FLOPS = 2 * S * D * 2 * F + 2 * S * P * F * F
+
+F32 = mybir.dt.float32
+BF16 = mybir.dt.bfloat16
+I32 = mybir.dt.int32
+U32 = mybir.dt.uint32
+U8 = mybir.dt.uint8
+FP8 = mybir.dt.float8_e4m3fn
+FP8X4 = mybir.dt.float8_e4m3fn_x4
+FP4X4 = mybir.dt.float4_e2m1fn_x4
+ADD = mybir.AluOpType.add
+MULT = mybir.AluOpType.mult
+POW = mybir.AluOpType.pow
+ACT = mybir.ActivationFunctionType
+
+N = 512
+TILES = 2 * P
+GCH = 512
+
+
+def tile_film_modulated_projection_f7_kernel(
+    tc, cond_bytes, cond_scale, film_words, film_scales, film_bias, x, gain,
+    proj_words, proj_scales, proj_bias, out,
+):
+    nc = tc.nc
+    with ExitStack() as ctx:
+        keep = ctx.enter_context(tc.tile_pool(name="keep", bufs=1))
+        ring = ctx.enter_context(tc.tile_pool(name="ring", bufs=3))
+        psum = ctx.enter_context(tc.psum_pool(name="psum", bufs=2))
+        ctx.enter_context(tc.manual_schedule())
+
+        def const(name, shape, dtype):
+            return keep.tile(shape, dtype, name=name, tag=name, align_bytes=64)
+
+        def bank(tag, bufs):
+            return psum.tile([128, N], F32, name="bank_" + tag, tag=tag, bufs=bufs)
+
+        ident = const("ident", [128, 128], F32)
+        ident_b = const("ident_b", [128, 128], BF16)
+        neg_half = const("neg_half", [128, 2], F32)
+        vec = const("vec", [128, N], BF16)
+        csc = const("csc", [128, 4, 4], F32)
+        cb = [const("cond_raw%d" % h, [128, D], U8) for h in range(2)]
+        cw = [const("cond_wide%d" % h, [128, D], BF16) for h in range(2)]
+        cc = [const("cond_codes%d" % h, [128, 4 * 128], U32) for h in range(2)]
+        cs = [const("cond_planes%d" % h, [128, 4 * 128], U8) for h in range(2)]
+        w1 = const("w1", [128, 8, 2048], U8)
+        fs = const("fs", [128, 4, 2048], U8)
+        w2 = const("w2", [128, 2, F], U32)
+        ps = const("ps", [128, 2, F], U8)
+        xs = const("xs", [128, TILES, F], BF16)
+        fb1 = const("fb1", [128, F], F32)
+        fbb = const("fbb", [128, F], F32)
+        gn = const("gn", [128, F], F32)
+        pb = const("pb", [128, F], F32)
+        gsb = [const("gsb%d" % h, [128, F], F32) for h in range(2)]
+        bsb = [const("bsb%d" % h, [128, F], F32) for h in range(2)]
+        ssq = const("ssq", [128, TILES], F32)
+        msq = const("msq", [128, TILES], F32)
+        rstd = const("rstd", [128, TILES], F32)
+
+        nc.gpsimd.dma_start(out=csc[:], in_=cond_scale.rearrange("o (g p t) -> p (o g) t", p=128, t=4))
+        nc.vector.memset(vec[:], 0.0)
+        nc.vector.memset(fs[:].rearrange("p g n -> p (g n)").bitcast(I32), 0)
+        nc.vector.memset(ps[:].rearrange("p g n -> p (g n)").bitcast(I32), 0)
+        nc.vector.memset(neg_half[:], -0.5)
+        make_identity(nc, ident[:])
+
+        nc.sync.dma_start(out=cb[0][:], in_=cond_bytes[0:128, :])
+        nc.scalar.dma_start(out=vec[0:4, :], in_=film_bias.rearrange("(c n) -> c n", n=N))
+        nc.scalar.dma_start(out=vec[4:6, :], in_=gain.rearrange("(c n) -> c n", n=N))
+        nc.gpsimd.dma_start(out=vec[6:8, :], in_=proj_bias.rearrange("(c n) -> c n", n=N))
+        fsi = fs[:].bitcast(I32)
+        fsd = film_scales.bitcast(I32)
+        for q in range(4):
+            nc.scalar.dma_start(out=fsi[32 * q : 32 * q + 4, :, :], in_=fsd[:, 4 * q : 4 * q + 4, :].rearrange("g q n -> q g n"))
+        w1i = w1[:].bitcast(I32)
+        w1d = film_words.bitcast(I32)
+
+        def load_w1(half):
+            for g in range(4):
+                nc.sync.dma_start(out=w1i[:, 4 * half + g, :], in_=w1d[g, :, 512 * half : 512 * half + 512])
+
+        def load_x(pair):
+            half, j = divmod(2 * pair, P)
+            nc.sync.dma_start(out=xs[:, 2 * pair : 2 * pair + 2, :], in_=x[128 * half : 128 * half + 128, j : j + 2, :])
+
+        load_w1(0)
+        load_x(0)
+        load_w1(1)
+        nc.sync.dma_start(out=cb[1][:], in_=cond_bytes[128:256, :])
+        load_x(1)
+        psi = ps[:].bitcast(I32)
+        psd = proj_scales.bitcast(I32)
+        for q in range(4):
+            nc.sync.dma_start(out=psi[32 * q : 32 * q + 4, :, :], in_=psd[:, 4 * q : 4 * q + 4, :].rearrange("g q n -> q g n"))
+        w2d = proj_words.rearrange("g p n t -> g p (n t)").bitcast(I32)
+        for g in range(2):
+            nc.sync.dma_start(out=w2[:, g, :].bitcast(I32), in_=w2d[g])
+        for pair in range(2, 8):
+            load_x(pair)
+
+        def spread(c, tag, bufs):
+            b = bank(tag, bufs)
+            nc.tensor.matmul(b[:], lhsT=ident_b[:, c : c + 1].to_broadcast([128, 128]), rhs=vec[:], start=True, stop=True)
+            return b
+
+        def by_t(ap):
+            return ap.rearrange("q (p t) -> q t p", t=4)
+
+        def t_major(ap):
+            return ap.rearrange("q (t p) -> q t p", t=4)
+
+        def cols(n):
+            return slice(N * n, N * n + N)
+
+        def cond_cast(h, g):
+            nc.scalar.copy(out=cw[h][:, cols(g)], in_=cb[h][:, cols(g)].bitcast(FP8))
+
+        def cond_turn(h, g, tag, bufs):
+            words = cw[h][:].bitcast(F32)
+            b = bank(tag, bufs)
+            for u in range(2):
+                nc.tensor.transpose(b[:, 128 * u : 128 * u + 128], words[:, 256 * g + u : 256 * g + 256 : 2], ident[:])
+            return b
+
+        def cond_scale_quant(h, g, b):
+            t = ring.tile([128, 128, 4], BF16, name="cq", tag="cq", bufs=2, align_bytes=64)
+            src = b[:, 0:256].bitcast(BF16).rearrange("p (u s e) -> p s u e", u=2, e=2)
+            dst = t[:].rearrange("p s (u e) -> p s u e", u=2)
+            sc = csc[:, g, :].rearrange("p (u e) -> p u e", u=2).unsqueeze(1).to_broadcast([128, 128, 2, 2])
+            nc.vector.tensor_tensor(out=dst, in0=src, in1=sc, op=MULT)
+            nc.vector.quantize_mx(
+                out=cc[h][:, 128 * g : 128 * g + 128].bitcast(FP8X4),
+                scales=cs[h][:, 128 * g : 128 * g + 128],
+                in_=t[:].rearrange("p s t -> p (s t)"),
+            )
+
+        def film(h, part):
+            banks = [bank("y", 4), bank("y", 4)]
+            for g in range(4):
+                for n in range(2):
+                    nc.tensor.matmul_mx(
+                        out=banks[n][:],
+                        lhsT=cc[h][:, 128 * g : 128 * g + 128].bitcast(FP8X4),
+                        lhsT_scale=cs[h][:, 128 * g : 128 * g + 128],
+                        rhs=w1[:, 4 * part + g, 1024 * n : 1024 * n + 1024].bitcast(FP4X4),
+                        rhs_scale=fs[:, g, 1024 * part + N * n : 1024 * part + N * n + N],
+                        start=(g == 0),
+                        stop=(g == 3),
+                    )
+            return banks
+
+        def make_gain(h, banks):
+            for n in range(2):
+                t = ring.tile([128, N], F32, name="g1", tag="g1", bufs=2, align_bytes=64)
+                nc.vector.tensor_tensor(out=t_major(t[:]), in0=by_t(banks[n][:]), in1=t_major(fb1[:, cols(n)]), op=ADD)
+                nc.vector.tensor_tensor(out=gsb[h][:, cols(n)], in0=t[:], in1=gn[:, cols(n)], op=MULT)
+
+        def gain_to_psum(h):
+            banks = []
+            for n in range(2):
+                b = bank("g", 2)
+                nc.tensor.matmul(b[:], lhsT=ident[:], rhs=gsb[h][:, cols(n)], start=True, stop=True)
+                banks.append(b)
+            return banks
+
+        def make_shift(h, banks):
+            for n in range(2):
+                nc.vector.tensor_tensor(out=t_major(bsb[h][:, cols(n)]), in0=by_t(banks[n][:]), in1=t_major(fbb[:, cols(n)]), op=ADD)
+
+        def square(i):
+            junk = ring.tile([128, F], BF16, name="junk", tag="junk", bufs=2, align_bytes=64)
+            nc.scalar.activation(out=junk[:], in_=xs[:, i, :], func=ACT.Square, accum_out=ssq[:, i : i + 1])
+
+        def inv_root(i):
+            c = slice(i, i + 2)
+            nc.gpsimd.tensor_scalar(msq[:, c], ssq[:, c], 1.0 / F, 0.1, MULT, ADD)
+            nc.gpsimd.tensor_tensor(out=rstd[:, c], in0=msq[:, c], in1=neg_half[:], op=POW)
+
+        def add_bias(i):
+            t = ring.tile([128, F], F32, name="xb", tag="xb", bufs=5, align_bytes=64)
+            for c in range(0, F, GCH):
+                nc.gpsimd.tensor_tensor(out=t[:, c : c + GCH], in0=xs[:, i, c : c + GCH], in1=pb[:, c : c + GCH], op=ADD)
+            return t
+
+        def modulate(i, g_banks):
+            u = ring.tile([128, F], F32, name="u", tag="u", bufs=3, align_bytes=64)
+            for n in range(2):
+                nc.vector.scalar_tensor_tensor(
+                    out=t_major(u[:, cols(n)]), in0=by_t(xs[:, i, cols(n)]), scalar=rstd[:, i : i + 1],
+                    in1=t_major(g_banks[n][:]), op0=MULT, op1=MULT,
+                )
+            return u
+
+        def turn(i, u):
+            h = i // P
+            banks = []
+            for n in range(2):
+                b = bank("t", 2)
+                for t in range(4):
+                    o = b[:, 128 * t : 128 * t + 128]
+                    c = slice(N * n + 128 * t, N * n + 128 * t + 128)
+                    nc.tensor.matmul(o, lhsT=u[:, c], rhs=ident[:], start=True, stop=False, is_transpose=True)
+                    nc.tensor.matmul(o, lhsT=bsb[h][:, c], rhs=ident[:], start=False, stop=True, is_transpose=True)
+                banks.append(b)
+            return banks
+
+        def relu(banks):
+            hq = ring.tile([128, 2, 128, 4], BF16, name="hq", tag="hq", bufs=2, align_bytes=64)
+            for n in range(2):
+                nc.scalar.activation(out=hq[:, n, :, :], in_=banks[n][:].rearrange("p (t s) -> p s t", t=4), func=ACT.Relu)
+            return hq
+
+        def quant(hq):
+            hc = ring.tile([128, 256], U32, name="hc", tag="hc", bufs=3, align_bytes=64)
+            hs = ring.tile([128, 256], U8, name="hs", tag="hs", bufs=3, align_bytes=64)
+            nc.vector.quantize_mx(out=hc[:].bitcast(FP8X4), scales=hs[:], in_=hq[:].rearrange("p g s t -> p (g s t)"))
+            return hc, hs
+
+        def project(codes):
+            hc, hs = codes
+            banks = []
+            for n in range(2):
+                b = bank("y", 4)
+                for g in range(2):
+                    nc.tensor.matmul_mx(
+                        out=b[:],
+                        lhsT=hc[:, 128 * g : 128 * g + 128].bitcast(FP8X4),
+                        lhsT_scale=hs[:, 128 * g : 128 * g + 128],
+                        rhs=w2[:, g, cols(n)].bitcast(FP8X4),
+                        rhs_scale=ps[:, g, cols(n)],
+                        start=(g == 0),
+                        stop=(g == 1),
+                    )
+                banks.append(b)
+            return banks
+
+        def finish(i, banks, xb):
+            o = ring.tile([128, F], F32, name="o", tag="o", bufs=4, align_bytes=64)
+            h, j = divmod(i, P)
+            dst = out[128 * h : 128 * h + 128, j, :]
+            for n in range(2):
+                nc.vector.tensor_tensor(out=o[:, cols(n)], in0=banks[n][:], in1=xb[:, cols(n)], op=ADD)
+                if i == TILES - 1:
+                    nc.sync.dma_start(out=dst[:, cols(n)], in_=o[:, cols(n)])
+            if i < TILES - 1:
+                nc.sync.dma_start(out=dst, in_=o[:])
+
+        nc.vector.tensor_copy(out=ident_b[:], in_=ident[:])
+        fg = [spread(0, "y", 4), spread(1, "y", 4)]
+        gb = [spread(4, "g", 2), spread(5, "g", 2)]
+        for n in range(2):
+            nc.vector.tensor_scalar(t_major(fb1[:, cols(n)]), by_t(fg[n][:]), 1.0, None, ADD)
+        for g in range(4):
+            cond_cast(0, g)
+        for g in range(4):
+            b = cond_turn(0, g, "t", 2)
+            cond_scale_quant(0, g, b)
+        pbb = [spread(6, "y", 4), spread(7, "y", 4)]
+        for n in range(2):
+            nc.scalar.copy(out=pb[:, cols(n)], in_=pbb[n][:])
+        for n in range(2):
+            nc.scalar.copy(out=t_major(gn[:, cols(n)]), in_=by_t(gb[n][:]))
+        fbk = [spread(2, "t", 2), spread(3, "t", 2)]
+        xb = {0: add_bias(0)}
+        square(0)
+        square(1)
+        inv_root(0)
+        gamma = film(0, 0)
+        for n in range(2):
+            nc.scalar.copy(out=t_major(fbb[:, cols(n)]), in_=by_t(fbk[n][:]))
+        make_gain(0, gamma)
+        g_banks = gain_to_psum(0)
+        beta = film(0, 1)
+        u = {0: modulate(0, g_banks)}
+        make_shift(0, beta)
+        square(2)
+        square(3)
+        inv_root(2)
+
+        cond_banks = {}
+        codes = {}
+        y = {}
+        for s in range(TILES + 2):
+            if s < TILES:
+                tb = turn(s, u.pop(s))
+                hq = relu(tb)
+            if 1 <= s <= TILES:
+                y[s - 1] = project(codes.pop(s - 1))
+            if s < 2:
+                for g in (2 * s, 2 * s + 1):
+                    cond_cast(1, g)
+                    cond_banks[g] = cond_turn(1, g, "y", 4)
+            if s == 3:
+                gamma = film(1, 0)
+            if s == 5:
+                beta = film(1, 1)
+            if s + 4 < TILES:
+                square(s + 4)
+                if s % 2 == 1:
+                    inv_root(s + 3)
+            if s + 1 < TILES:
+                u[s + 1] = modulate(s + 1, g_banks)
+            if s >= 2:
+                finish(s - 2, y.pop(s - 2), xb.pop(s - 2))
+            if s < TILES:
+                codes[s] = quant(hq)
+            if s + 1 < TILES:
+                xb[s + 1] = add_bias(s + 1)
+            if s < 2:
+                for g in (2 * s, 2 * s + 1):
+                    cond_scale_quant(1, g, cond_banks.pop(g))
+            if s == 4:
+                make_gain(1, gamma)
+            if s == 6:
+                make_shift(1, beta)
+                g_banks = gain_to_psum(1)

@@ -67,19 +67,19 @@ def tile_film_modulated_projection_f7_kernel(
 
         nc.gpsimd.dma_start(out=csc[:], in_=cond_scale.rearrange("o (g p t) -> p (o g) t", p=128, t=4))
         nc.vector.memset(vec[:], 0.0)
+        nc.scalar.activation(out=rstd[:, 0:1], in_=vec[:, 0:1], func=ACT.Square)
         nc.vector.memset(fs[:].rearrange("p g n -> p (g n)").bitcast(I32), 0)
-        nc.vector.memset(ps[:].rearrange("p g n -> p (g n)").bitcast(I32), 0)
-        nc.vector.memset(neg_half[:], -0.5)
         make_identity(nc, ident[:])
+        nc.gpsimd.memset(neg_half[:], -0.5)
+        nc.vector.tensor_copy(out=ident_b[:], in_=ident[:])
+        nc.vector.memset(ps[:].rearrange("p g n -> p (g n)").bitcast(I32), 0)
 
         nc.sync.dma_start(out=cb[0][:], in_=cond_bytes[0:128, :])
-        nc.scalar.dma_start(out=vec[0:4, :], in_=film_bias.rearrange("(c n) -> c n", n=N))
-        nc.scalar.dma_start(out=vec[4:6, :], in_=gain.rearrange("(c n) -> c n", n=N))
-        nc.gpsimd.dma_start(out=vec[6:8, :], in_=proj_bias.rearrange("(c n) -> c n", n=N))
+        nc.sync.dma_start(out=vec[0:4, :], in_=film_bias.rearrange("(c n) -> c n", n=N))
+        nc.sync.dma_start(out=vec[4:6, :], in_=gain.rearrange("(c n) -> c n", n=N))
+        nc.sync.dma_start(out=vec[6:8, :], in_=proj_bias.rearrange("(c n) -> c n", n=N))
         fsi = fs[:].bitcast(I32)
         fsd = film_scales.bitcast(I32)
-        for q in range(4):
-            nc.scalar.dma_start(out=fsi[32 * q : 32 * q + 4, :, :], in_=fsd[:, 4 * q : 4 * q + 4, :].rearrange("g q n -> q g n"))
         w1i = w1[:].bitcast(I32)
         w1d = film_words.bitcast(I32)
 
@@ -92,8 +92,10 @@ def tile_film_modulated_projection_f7_kernel(
             nc.sync.dma_start(out=xs[:, 2 * pair : 2 * pair + 2, :], in_=x[128 * half : 128 * half + 128, j : j + 2, :])
 
         load_w1(0)
-        load_x(0)
+        for q in range(4):
+            nc.sync.dma_start(out=fsi[32 * q : 32 * q + 4, :, :], in_=fsd[:, 4 * q : 4 * q + 4, :].rearrange("g q n -> q g n"))
         load_w1(1)
+        load_x(0)
         nc.sync.dma_start(out=cb[1][:], in_=cond_bytes[128:256, :])
         load_x(1)
         psi = ps[:].bitcast(I32)
@@ -142,10 +144,10 @@ def tile_film_modulated_projection_f7_kernel(
                 in_=t[:].rearrange("p s t -> p (s t)"),
             )
 
-        def film(h, part):
-            banks = [bank("y", 4), bank("y", 4)]
+        def film(h, part, halves):
+            banks = {n: bank("y", 4) for n in halves}
             for g in range(4):
-                for n in range(2):
+                for n in halves:
                     nc.tensor.matmul_mx(
                         out=banks[n][:],
                         lhsT=cc[h][:, 128 * g : 128 * g + 128].bitcast(FP8X4),
@@ -157,23 +159,18 @@ def tile_film_modulated_projection_f7_kernel(
                     )
             return banks
 
-        def make_gain(h, banks):
-            for n in range(2):
-                t = ring.tile([128, N], F32, name="g1", tag="g1", bufs=2, align_bytes=64)
-                nc.vector.tensor_tensor(out=t_major(t[:]), in0=by_t(banks[n][:]), in1=t_major(fb1[:, cols(n)]), op=ADD)
-                nc.vector.tensor_tensor(out=gsb[h][:, cols(n)], in0=t[:], in1=gn[:, cols(n)], op=MULT)
+        def make_gain(h, n, b):
+            t = ring.tile([128, N], F32, name="g1", tag="g1", bufs=2, align_bytes=64)
+            nc.vector.tensor_tensor(out=t_major(t[:]), in0=by_t(b[:]), in1=t_major(fb1[:, cols(n)]), op=ADD)
+            nc.vector.tensor_tensor(out=gsb[h][:, cols(n)], in0=t[:], in1=gn[:, cols(n)], op=MULT)
 
-        def gain_to_psum(h):
-            banks = []
-            for n in range(2):
-                b = bank("g", 2)
-                nc.tensor.matmul(b[:], lhsT=ident[:], rhs=gsb[h][:, cols(n)], start=True, stop=True)
-                banks.append(b)
-            return banks
+        def gain_to_psum(h, n):
+            b = bank("g", 2)
+            nc.tensor.matmul(b[:], lhsT=ident[:], rhs=gsb[h][:, cols(n)], start=True, stop=True)
+            return b
 
-        def make_shift(h, banks):
-            for n in range(2):
-                nc.vector.tensor_tensor(out=t_major(bsb[h][:, cols(n)]), in0=by_t(banks[n][:]), in1=t_major(fbb[:, cols(n)]), op=ADD)
+        def make_shift(h, n, b):
+            nc.vector.tensor_tensor(out=t_major(bsb[h][:, cols(n)]), in0=by_t(b[:]), in1=t_major(fbb[:, cols(n)]), op=ADD)
 
         def square(i):
             junk = ring.tile([128, F], BF16, name="junk", tag="junk", bufs=2, align_bytes=64)
@@ -199,24 +196,17 @@ def tile_film_modulated_projection_f7_kernel(
                 )
             return u
 
-        def turn(i, u):
-            h = i // P
-            banks = []
-            for n in range(2):
-                b = bank("t", 2)
-                for t in range(4):
-                    o = b[:, 128 * t : 128 * t + 128]
-                    c = slice(N * n + 128 * t, N * n + 128 * t + 128)
-                    nc.tensor.matmul(o, lhsT=u[:, c], rhs=ident[:], start=True, stop=False, is_transpose=True)
-                    nc.tensor.matmul(o, lhsT=bsb[h][:, c], rhs=ident[:], start=False, stop=True, is_transpose=True)
-                banks.append(b)
-            return banks
+        def turn(i, n, u):
+            b = bank("t", 2)
+            for t in range(4):
+                o = b[:, 128 * t : 128 * t + 128]
+                c = slice(N * n + 128 * t, N * n + 128 * t + 128)
+                nc.tensor.matmul(o, lhsT=u[:, c], rhs=ident[:], start=True, stop=False, is_transpose=True)
+                nc.tensor.matmul(o, lhsT=bsb[i // P][:, c], rhs=ident[:], start=False, stop=True, is_transpose=True)
+            return b
 
-        def relu(banks):
-            hq = ring.tile([128, 2, 128, 4], BF16, name="hq", tag="hq", bufs=2, align_bytes=64)
-            for n in range(2):
-                nc.scalar.activation(out=hq[:, n, :, :], in_=banks[n][:].rearrange("p (t s) -> p s t", t=4), func=ACT.Relu)
-            return hq
+        def relu(hq, n, b):
+            nc.scalar.activation(out=hq[:, n, :, :], in_=b[:].rearrange("p (t s) -> p s t", t=4), func=ACT.Relu)
 
         def quant(hq):
             hc = ring.tile([128, 256], U32, name="hc", tag="hc", bufs=3, align_bytes=64)
@@ -224,23 +214,20 @@ def tile_film_modulated_projection_f7_kernel(
             nc.vector.quantize_mx(out=hc[:].bitcast(FP8X4), scales=hs[:], in_=hq[:].rearrange("p g s t -> p (g s t)"))
             return hc, hs
 
-        def project(codes):
+        def project(codes, n):
             hc, hs = codes
-            banks = []
-            for n in range(2):
-                b = bank("y", 4)
-                for g in range(2):
-                    nc.tensor.matmul_mx(
-                        out=b[:],
-                        lhsT=hc[:, 128 * g : 128 * g + 128].bitcast(FP8X4),
-                        lhsT_scale=hs[:, 128 * g : 128 * g + 128],
-                        rhs=w2[:, g, cols(n)].bitcast(FP8X4),
-                        rhs_scale=ps[:, g, cols(n)],
-                        start=(g == 0),
-                        stop=(g == 1),
-                    )
-                banks.append(b)
-            return banks
+            b = bank("y", 4)
+            for g in range(2):
+                nc.tensor.matmul_mx(
+                    out=b[:],
+                    lhsT=hc[:, 128 * g : 128 * g + 128].bitcast(FP8X4),
+                    lhsT_scale=hs[:, 128 * g : 128 * g + 128],
+                    rhs=w2[:, g, cols(n)].bitcast(FP8X4),
+                    rhs_scale=ps[:, g, cols(n)],
+                    start=(g == 0),
+                    stop=(g == 1),
+                )
+            return b
 
         def finish(i, banks, xb):
             o = ring.tile([128, F], F32, name="o", tag="o", bufs=4, align_bytes=64)
@@ -253,72 +240,84 @@ def tile_film_modulated_projection_f7_kernel(
             if i < TILES - 1:
                 nc.sync.dma_start(out=dst, in_=o[:])
 
-        nc.vector.tensor_copy(out=ident_b[:], in_=ident[:])
         fg = [spread(0, "y", 4), spread(1, "y", 4)]
         gb = [spread(4, "g", 2), spread(5, "g", 2)]
-        for n in range(2):
-            nc.vector.tensor_scalar(t_major(fb1[:, cols(n)]), by_t(fg[n][:]), 1.0, None, ADD)
         for g in range(4):
             cond_cast(0, g)
+        for n in range(2):
+            nc.vector.tensor_scalar(t_major(fb1[:, cols(n)]), by_t(fg[n][:]), 1.0, None, ADD)
         for g in range(4):
             b = cond_turn(0, g, "t", 2)
             cond_scale_quant(0, g, b)
         pbb = [spread(6, "y", 4), spread(7, "y", 4)]
+        fbk = [spread(2, "t", 2), spread(3, "t", 2)]
+        for n in range(2):
+            nc.scalar.copy(out=t_major(gn[:, cols(n)]), in_=by_t(gb[n][:]))
         for n in range(2):
             nc.scalar.copy(out=pb[:, cols(n)], in_=pbb[n][:])
         for n in range(2):
-            nc.scalar.copy(out=t_major(gn[:, cols(n)]), in_=by_t(gb[n][:]))
-        fbk = [spread(2, "t", 2), spread(3, "t", 2)]
-        xb = {0: add_bias(0)}
+            nc.scalar.copy(out=t_major(fbb[:, cols(n)]), in_=by_t(fbk[n][:]))
+        gamma = film(0, 0, (0, 1))
+        for n in range(2):
+            make_gain(0, n, gamma[n])
+        beta = film(0, 1, (0, 1))
+        g_banks = [gain_to_psum(0, n) for n in range(2)]
+        for n in range(2):
+            make_shift(0, n, beta[n])
         square(0)
         square(1)
+        xb = {0: add_bias(0)}
         inv_root(0)
-        gamma = film(0, 0)
-        for n in range(2):
-            nc.scalar.copy(out=t_major(fbb[:, cols(n)]), in_=by_t(fbk[n][:]))
-        make_gain(0, gamma)
-        g_banks = gain_to_psum(0)
-        beta = film(0, 1)
         u = {0: modulate(0, g_banks)}
-        make_shift(0, beta)
+        for g in range(4):
+            cond_cast(1, g)
         square(2)
         square(3)
+        xb[1] = add_bias(1)
         inv_root(2)
 
         cond_banks = {}
+        hqs = {}
         codes = {}
         y = {}
-        for s in range(TILES + 2):
-            if s < TILES:
-                tb = turn(s, u.pop(s))
-                hq = relu(tb)
-            if 1 <= s <= TILES:
-                y[s - 1] = project(codes.pop(s - 1))
-            if s < 2:
-                for g in (2 * s, 2 * s + 1):
-                    cond_cast(1, g)
-                    cond_banks[g] = cond_turn(1, g, "y", 4)
-            if s == 3:
-                gamma = film(1, 0)
-            if s == 5:
-                beta = film(1, 1)
+        g_next = []
+        for s in range(TILES + 3):
             if s + 4 < TILES:
                 square(s + 4)
                 if s % 2 == 1:
                     inv_root(s + 3)
-            if s + 1 < TILES:
-                u[s + 1] = modulate(s + 1, g_banks)
-            if s >= 2:
-                finish(s - 2, y.pop(s - 2), xb.pop(s - 2))
             if s < TILES:
-                codes[s] = quant(hq)
-            if s + 1 < TILES:
-                xb[s + 1] = add_bias(s + 1)
+                hqs[s] = ring.tile([128, 2, 128, 4], BF16, name="hq", tag="hq", bufs=3, align_bytes=64)
+            for n in range(2):
+                if s < TILES:
+                    b = turn(s, n, u[s])
+                    relu(hqs[s], n, b)
+                if s < 2:
+                    g = 2 * s + n
+                    cond_banks[g] = cond_turn(1, g, "y", 4)
+                if s == 7:
+                    g_next.append(gain_to_psum(1, n))
+                if 2 <= s < TILES + 2:
+                    y[s - 2, n] = project(codes[s - 2], n)
+            if s == 3 or s == 4:
+                gamma[s - 3] = film(1, 0, (s - 3,))[s - 3]
+            if s == 5 or s == 6:
+                beta[s - 5] = film(1, 1, (s - 5,))[s - 5]
+            if s + 1 < TILES and s != 7:
+                u[s + 1] = modulate(s + 1, g_banks)
+            if 1 <= s <= TILES:
+                codes[s - 1] = quant(hqs.pop(s - 1))
+            if s >= 3:
+                finish(s - 3, [y.pop((s - 3, 0)), y.pop((s - 3, 1))], xb.pop(s - 3))
+            if s == 7:
+                g_banks = g_next
+                u[s + 1] = modulate(s + 1, g_banks)
             if s < 2:
                 for g in (2 * s, 2 * s + 1):
                     cond_scale_quant(1, g, cond_banks.pop(g))
-            if s == 4:
-                make_gain(1, gamma)
-            if s == 6:
-                make_shift(1, beta)
-                g_banks = gain_to_psum(1)
+            if s == 4 or s == 5:
+                make_gain(1, s - 4, gamma[s - 4])
+            if s == 6 or s == 7:
+                make_shift(1, s - 6, beta[s - 6])
+            if s + 2 < TILES:
+                xb[s + 2] = add_bias(s + 2)

@@ -21,7 +21,6 @@ ACT = mybir.ActivationFunctionType
 
 N = 512
 TILES = 2 * P
-GCH = 512
 
 
 def tile_film_modulated_projection_f7_kernel(
@@ -122,8 +121,8 @@ def tile_film_modulated_projection_f7_kernel(
         def cols(n):
             return slice(N * n, N * n + N)
 
-        def cond_cast(h, g):
-            nc.scalar.copy(out=cw[h][:, cols(g)], in_=cb[h][:, cols(g)].bitcast(FP8))
+        def cond_cast(copy, h, g):
+            copy(out=cw[h][:, cols(g)], in_=cb[h][:, cols(g)].bitcast(FP8))
 
         def cond_turn(h, g, tag, bufs):
             words = cw[h][:].bitcast(F32)
@@ -144,10 +143,10 @@ def tile_film_modulated_projection_f7_kernel(
                 in_=t[:].rearrange("p s t -> p (s t)"),
             )
 
-        def film(h, part, halves):
-            banks = {n: bank("y", 4) for n in halves}
+        def film(h, part):
+            banks = [bank("y", 4), bank("y", 4)]
             for g in range(4):
-                for n in halves:
+                for n in range(2):
                     nc.tensor.matmul_mx(
                         out=banks[n][:],
                         lhsT=cc[h][:, 128 * g : 128 * g + 128].bitcast(FP8X4),
@@ -182,13 +181,15 @@ def tile_film_modulated_projection_f7_kernel(
             nc.gpsimd.tensor_tensor(out=rstd[:, c], in0=msq[:, c], in1=neg_half[:], op=POW)
 
         def add_bias(i):
-            t = ring.tile([128, F], F32, name="xb", tag="xb", bufs=5, align_bytes=64)
-            for c in range(0, F, GCH):
-                nc.gpsimd.tensor_tensor(out=t[:, c : c + GCH], in0=xs[:, i, c : c + GCH], in1=pb[:, c : c + GCH], op=ADD)
-            return t
+            pair = []
+            for n in range(2):
+                t = ring.tile([128, N], F32, name="xb%d" % n, tag="xb%d" % n, bufs=4, align_bytes=64)
+                nc.gpsimd.tensor_tensor(out=t[:], in0=xs[:, i, cols(n)], in1=pb[:, cols(n)], op=ADD)
+                pair.append(t)
+            return pair
 
         def modulate(i, g_banks):
-            u = ring.tile([128, F], F32, name="u", tag="u", bufs=3, align_bytes=64)
+            u = ring.tile([128, F], F32, name="u", tag="u", bufs=4, align_bytes=64)
             for n in range(2):
                 nc.vector.scalar_tensor_tensor(
                     out=t_major(u[:, cols(n)]), in0=by_t(xs[:, i, cols(n)]), scalar=rstd[:, i : i + 1],
@@ -229,26 +230,32 @@ def tile_film_modulated_projection_f7_kernel(
                 )
             return b
 
-        def finish(i, banks, xb):
-            o = ring.tile([128, F], F32, name="o", tag="o", bufs=4, align_bytes=64)
+        outs = {}
+
+        def finish(i, n, b, xb):
+            if n == 0:
+                outs[i] = ring.tile([128, F], F32, name="o", tag="o", bufs=4, align_bytes=64)
+            o = outs[i]
             h, j = divmod(i, P)
             dst = out[128 * h : 128 * h + 128, j, :]
-            for n in range(2):
-                nc.vector.tensor_tensor(out=o[:, cols(n)], in0=banks[n][:], in1=xb[:, cols(n)], op=ADD)
-                if i == TILES - 1:
-                    nc.sync.dma_start(out=dst[:, cols(n)], in_=o[:, cols(n)])
-            if i < TILES - 1:
+            nc.vector.tensor_tensor(out=o[:, cols(n)], in0=b[:], in1=xb[n][:], op=ADD)
+            if i == TILES - 1:
+                nc.sync.dma_start(out=dst[:, cols(n)], in_=o[:, cols(n)])
+            elif n == 1:
                 nc.sync.dma_start(out=dst, in_=o[:])
 
-        fg = [spread(0, "y", 4), spread(1, "y", 4)]
-        gb = [spread(4, "g", 2), spread(5, "g", 2)]
         for g in range(4):
-            cond_cast(0, g)
-        for n in range(2):
-            nc.vector.tensor_scalar(t_major(fb1[:, cols(n)]), by_t(fg[n][:]), 1.0, None, ADD)
+            cond_cast((nc.scalar.copy, nc.vector.tensor_copy)[g % 2], 0, g)
         for g in range(4):
             b = cond_turn(0, g, "t", 2)
             cond_scale_quant(0, g, b)
+            if g == 1:
+                fg = [spread(0, "y", 4), spread(1, "y", 4)]
+            if g == 3:
+                gb = [spread(4, "g", 2), spread(5, "g", 2)]
+        for n in range(2):
+            nc.vector.tensor_scalar(t_major(fb1[:, cols(n)]), by_t(fg[n][:]), 1.0, None, ADD)
+        gamma = film(0, 0)
         pbb = [spread(6, "y", 4), spread(7, "y", 4)]
         fbk = [spread(2, "t", 2), spread(3, "t", 2)]
         for n in range(2):
@@ -257,10 +264,11 @@ def tile_film_modulated_projection_f7_kernel(
             nc.scalar.copy(out=pb[:, cols(n)], in_=pbb[n][:])
         for n in range(2):
             nc.scalar.copy(out=t_major(fbb[:, cols(n)]), in_=by_t(fbk[n][:]))
-        gamma = film(0, 0, (0, 1))
         for n in range(2):
             make_gain(0, n, gamma[n])
-        beta = film(0, 1, (0, 1))
+        for g in range(4):
+            cond_cast(nc.vector.tensor_copy, 1, g)
+        beta = film(0, 1)
         g_banks = [gain_to_psum(0, n) for n in range(2)]
         for n in range(2):
             make_shift(0, n, beta[n])
@@ -269,12 +277,11 @@ def tile_film_modulated_projection_f7_kernel(
         xb = {0: add_bias(0)}
         inv_root(0)
         u = {0: modulate(0, g_banks)}
-        for g in range(4):
-            cond_cast(1, g)
         square(2)
         square(3)
-        xb[1] = add_bias(1)
         inv_root(2)
+        xb[1] = add_bias(1)
+        u[1] = modulate(1, g_banks)
 
         cond_banks = {}
         hqs = {}
@@ -290,34 +297,33 @@ def tile_film_modulated_projection_f7_kernel(
                 hqs[s] = ring.tile([128, 2, 128, 4], BF16, name="hq", tag="hq", bufs=3, align_bytes=64)
             for n in range(2):
                 if s < TILES:
-                    b = turn(s, n, u[s])
-                    relu(hqs[s], n, b)
-                if s < 2:
-                    g = 2 * s + n
-                    cond_banks[g] = cond_turn(1, g, "y", 4)
-                if s == 7:
+                    relu(hqs[s], n, turn(s, n, u[s]))
+                if s == 0:
+                    for g in (2 * n, 2 * n + 1):
+                        cond_banks[g] = cond_turn(1, g, "y", 4)
+                if s == 6:
                     g_next.append(gain_to_psum(1, n))
                 if 2 <= s < TILES + 2:
                     y[s - 2, n] = project(codes[s - 2], n)
-            if s == 3 or s == 4:
-                gamma[s - 3] = film(1, 0, (s - 3,))[s - 3]
-            if s == 5 or s == 6:
-                beta[s - 5] = film(1, 1, (s - 5,))[s - 5]
-            if s + 1 < TILES and s != 7:
-                u[s + 1] = modulate(s + 1, g_banks)
+            if s == 1:
+                gamma = film(1, 0)
+                beta = film(1, 1)
+            if s == 6:
+                g_banks = g_next
+            if s >= 3:
+                for n in range(2):
+                    finish(s - 3, n, y.pop((s - 3, n)), xb[s - 3])
             if 1 <= s <= TILES:
                 codes[s - 1] = quant(hqs.pop(s - 1))
-            if s >= 3:
-                finish(s - 3, [y.pop((s - 3, 0)), y.pop((s - 3, 1))], xb.pop(s - 3))
-            if s == 7:
-                g_banks = g_next
-                u[s + 1] = modulate(s + 1, g_banks)
-            if s < 2:
-                for g in (2 * s, 2 * s + 1):
-                    cond_scale_quant(1, g, cond_banks.pop(g))
-            if s == 4 or s == 5:
-                make_gain(1, s - 4, gamma[s - 4])
-            if s == 6 or s == 7:
-                make_shift(1, s - 6, beta[s - 6])
             if s + 2 < TILES:
-                xb[s + 2] = add_bias(s + 2)
+                u[s + 2] = modulate(s + 2, g_banks)
+            if s == 0:
+                for g in range(4):
+                    cond_scale_quant(1, g, cond_banks.pop(g))
+            if s == 1:
+                for n in range(2):
+                    make_gain(1, n, gamma[n])
+                for n in range(2):
+                    make_shift(1, n, beta[n])
+            if 2 <= s + 1 < TILES:
+                xb[s + 1] = add_bias(s + 1)

@@ -21,6 +21,7 @@ ACT = mybir.ActivationFunctionType
 
 N = 512
 TILES = 2 * P
+ON_SCALAR = (6, 8, 10, 12, 14)
 
 
 def tile_film_modulated_projection_f7_kernel(
@@ -43,7 +44,12 @@ def tile_film_modulated_projection_f7_kernel(
         ident = const("ident", [128, 128], F32)
         ident_b = const("ident_b", [128, 128], BF16)
         neg_half = const("neg_half", [128, 2], F32)
+        turn_fwd = const("turn_fwd", [128, 128], F32)
+        sc = const("sc", [128, N], F32)
+        vt = const("vt", [128, 128], BF16)
         vec = const("vec", [128, N], BF16)
+        gcol = const("gcol", [128, 8], F32)
+        g1col = const("g1col", [128, 8], F32)
         csc = const("csc", [128, 4, 4], F32)
         cb = [const("cond_raw%d" % h, [128, D], U8) for h in range(2)]
         cw = [const("cond_wide%d" % h, [128, D], BF16) for h in range(2)]
@@ -54,29 +60,31 @@ def tile_film_modulated_projection_f7_kernel(
         w2 = const("w2", [128, 2, F], U32)
         ps = const("ps", [128, 2, F], U8)
         xs = const("xs", [128, TILES, F], BF16)
-        fb1 = const("fb1", [128, F], F32)
         fbb = const("fbb", [128, F], F32)
-        gn = const("gn", [128, F], F32)
         pb = const("pb", [128, F], F32)
-        gsb = [const("gsb%d" % h, [128, F], F32) for h in range(2)]
+        gts = [const("gts%d" % h, [128, F], F32) for h in range(2)]
         bsb = [const("bsb%d" % h, [128, F], F32) for h in range(2)]
         ssq = const("ssq", [128, TILES], F32)
         msq = const("msq", [128, TILES], F32)
         rstd = const("rstd", [128, TILES], F32)
 
-        nc.gpsimd.dma_start(out=csc[:], in_=cond_scale.rearrange("o (g p t) -> p (o g) t", p=128, t=4))
-        nc.vector.memset(vec[:], 0.0)
-        nc.scalar.activation(out=rstd[:, 0:1], in_=vec[:, 0:1], func=ACT.Square)
-        nc.vector.memset(fs[:].rearrange("p g n -> p (g n)").bitcast(I32), 0)
-        make_identity(nc, ident[:])
         nc.gpsimd.memset(neg_half[:], -0.5)
+        make_identity(nc, ident[:])
+        nc.vector.memset(sc[:], 0.0)
+        nc.vector.memset(vt[:], 0.0)
+        nc.vector.memset(vec[:], 0.0)
+        nc.vector.memset(fs[:].rearrange("p g n -> p (g n)").bitcast(I32), 0)
         nc.vector.tensor_copy(out=ident_b[:], in_=ident[:])
+        nc.vector.tensor_copy(out=turn_fwd[:].rearrange("q (t p) -> q t p", t=4), in_=ident[:].rearrange("q (p t) -> q t p", t=4))
         nc.vector.memset(ps[:].rearrange("p g n -> p (g n)").bitcast(I32), 0)
 
         nc.sync.dma_start(out=cb[0][:], in_=cond_bytes[0:128, :])
-        nc.sync.dma_start(out=vec[0:4, :], in_=film_bias.rearrange("(c n) -> c n", n=N))
-        nc.sync.dma_start(out=vec[4:6, :], in_=gain.rearrange("(c n) -> c n", n=N))
-        nc.sync.dma_start(out=vec[6:8, :], in_=proj_bias.rearrange("(c n) -> c n", n=N))
+        nc.scalar.dma_start(out=sc[0:4, :], in_=cond_scale.rearrange("o (g n) -> (o g) n", n=N))
+        nc.scalar.dma_start(out=vt[0:8, :], in_=gain.rearrange("(c m) -> c m", m=128))
+        nc.scalar.dma_start(out=vt[8:16, :], in_=film_bias[0:F].rearrange("(c m) -> c m", m=128))
+        nc.scalar.dma_start(out=vec[0:2, :], in_=film_bias[F : 2 * F].rearrange("(c n) -> c n", n=N))
+        nc.scalar.dma_start(out=vec[2:4, :], in_=proj_bias.rearrange("(c n) -> c n", n=N))
+        nc.scalar.activation(out=rstd[:, 0:1], in_=neg_half[:, 0:1], func=ACT.Square)
         fsi = fs[:].bitcast(I32)
         fsd = film_scales.bitcast(I32)
         w1i = w1[:].bitcast(I32)
@@ -93,9 +101,9 @@ def tile_film_modulated_projection_f7_kernel(
         load_w1(0)
         for q in range(4):
             nc.sync.dma_start(out=fsi[32 * q : 32 * q + 4, :, :], in_=fsd[:, 4 * q : 4 * q + 4, :].rearrange("g q n -> q g n"))
-        load_w1(1)
         load_x(0)
         nc.sync.dma_start(out=cb[1][:], in_=cond_bytes[128:256, :])
+        load_w1(1)
         load_x(1)
         psi = ps[:].bitcast(I32)
         psd = proj_scales.bitcast(I32)
@@ -143,7 +151,7 @@ def tile_film_modulated_projection_f7_kernel(
                 in_=t[:].rearrange("p s t -> p (s t)"),
             )
 
-        def film(h, part):
+        def film_beta(h):
             banks = [bank("y", 4), bank("y", 4)]
             for g in range(4):
                 for n in range(2):
@@ -151,21 +159,40 @@ def tile_film_modulated_projection_f7_kernel(
                         out=banks[n][:],
                         lhsT=cc[h][:, 128 * g : 128 * g + 128].bitcast(FP8X4),
                         lhsT_scale=cs[h][:, 128 * g : 128 * g + 128],
-                        rhs=w1[:, 4 * part + g, 1024 * n : 1024 * n + 1024].bitcast(FP4X4),
-                        rhs_scale=fs[:, g, 1024 * part + N * n : 1024 * part + N * n + N],
+                        rhs=w1[:, 4 + g, 1024 * n : 1024 * n + 1024].bitcast(FP4X4),
+                        rhs_scale=fs[:, g, F + N * n : F + N * n + N],
                         start=(g == 0),
                         stop=(g == 3),
                     )
             return banks
 
-        def make_gain(h, n, b):
-            t = ring.tile([128, N], F32, name="g1", tag="g1", bufs=2, align_bytes=64)
-            nc.vector.tensor_tensor(out=t_major(t[:]), in0=by_t(b[:]), in1=t_major(fb1[:, cols(n)]), op=ADD)
-            nc.vector.tensor_tensor(out=gsb[h][:, cols(n)], in0=t[:], in1=gn[:, cols(n)], op=MULT)
+        def film_gamma(h, n):
+            b = bank("y", 4)
+            for c in range(4 * n, 4 * n + 4):
+                for g in range(4):
+                    nc.tensor.matmul_mx(
+                        out=b[:, 128 * (c % 4) : 128 * (c % 4) + 128],
+                        lhsT=w1[:, g, 256 * c : 256 * c + 256].bitcast(FP4X4),
+                        lhsT_scale=fs[:, g, 128 * c : 128 * c + 128],
+                        rhs=cc[h][:, 128 * g : 128 * g + 128].bitcast(FP8X4),
+                        rhs_scale=cs[h][:, 128 * g : 128 * g + 128],
+                        start=(g == 0),
+                        stop=(g == 3),
+                    )
+            return b
 
-        def gain_to_psum(h, n):
+        def gain_rows(h, n, b):
+            for c in range(4 * n, 4 * n + 4):
+                nc.scalar.activation(
+                    out=gts[h][:, 128 * c : 128 * c + 128], in_=b[:, 128 * (c % 4) : 128 * (c % 4) + 128],
+                    func=ACT.Identity, scale=gcol[:, c : c + 1], bias=g1col[:, c : c + 1],
+                )
+
+        def gain_turn(h, n):
             b = bank("g", 2)
-            nc.tensor.matmul(b[:], lhsT=ident[:], rhs=gsb[h][:, cols(n)], start=True, stop=True)
+            for c in range(4):
+                k = N * n + 128 * c
+                nc.tensor.transpose(t_major(b[:])[:, :, 32 * c : 32 * c + 32], gts[h][:, k : k + 128], turn_fwd[:])
             return b
 
         def make_shift(h, n, b):
@@ -188,11 +215,16 @@ def tile_film_modulated_projection_f7_kernel(
                 pair.append(t)
             return pair
 
-        def modulate(i, g_banks):
+        def deinterleave(copy, i):
+            t = ring.tile([128, F], BF16, name="xd", tag="xd", bufs=4, align_bytes=64)
+            copy(out=t[:].rearrange("q (t c i) -> q c t i", t=4, i=8), in_=xs[:, i, :].rearrange("q (c i t) -> q c t i", t=4, i=8))
+            return t
+
+        def modulate(i, xd, g_banks):
             u = ring.tile([128, F], F32, name="u", tag="u", bufs=4, align_bytes=64)
             for n in range(2):
                 nc.vector.scalar_tensor_tensor(
-                    out=t_major(u[:, cols(n)]), in0=by_t(xs[:, i, cols(n)]), scalar=rstd[:, i : i + 1],
+                    out=t_major(u[:, cols(n)]), in0=xd[:].rearrange("q (t g p) -> q g t p", t=4, g=2)[:, n, :, :], scalar=rstd[:, i : i + 1],
                     in1=t_major(g_banks[n][:]), op0=MULT, op1=MULT,
                 )
             return u
@@ -244,70 +276,77 @@ def tile_film_modulated_projection_f7_kernel(
             elif n == 1:
                 nc.sync.dma_start(out=dst, in_=o[:])
 
+        tb = bank("t", 2)
+        for t in range(4):
+            nc.tensor.transpose(tb[:, 128 * t : 128 * t + 128], sc[:, t::4], ident[:])
+        nc.vector.tensor_copy(out=csc[:], in_=tb[:].rearrange("p (t r) -> p r t", t=4)[:, 0:4, :])
         for g in range(4):
             cond_cast((nc.scalar.copy, nc.vector.tensor_copy)[g % 2], 0, g)
         for g in range(4):
             b = cond_turn(0, g, "t", 2)
             cond_scale_quant(0, g, b)
             if g == 1:
-                fg = [spread(0, "y", 4), spread(1, "y", 4)]
-            if g == 3:
-                gb = [spread(4, "g", 2), spread(5, "g", 2)]
-        for n in range(2):
-            nc.vector.tensor_scalar(t_major(fb1[:, cols(n)]), by_t(fg[n][:]), 1.0, None, ADD)
-        gamma = film(0, 0)
-        pbb = [spread(6, "y", 4), spread(7, "y", 4)]
-        fbk = [spread(2, "t", 2), spread(3, "t", 2)]
-        for n in range(2):
-            nc.scalar.copy(out=t_major(gn[:, cols(n)]), in_=by_t(gb[n][:]))
-        for n in range(2):
-            nc.scalar.copy(out=pb[:, cols(n)], in_=pbb[n][:])
-        for n in range(2):
-            nc.scalar.copy(out=t_major(fbb[:, cols(n)]), in_=by_t(fbk[n][:]))
-        for n in range(2):
-            make_gain(0, n, gamma[n])
+                pbb = [spread(2, "y", 4), spread(3, "y", 4)]
+                vb = psum.tile([128, 2 * N], BF16, name="bank_v", tag="g", bufs=2)
+                nc.tensor.transpose(vb[:, 0:128], vt[:], ident_b[:])
+        nc.vector.tensor_copy(out=gcol[:], in_=vb[:, 0:8])
+        nc.vector.scalar_tensor_tensor(out=g1col[:], in0=vb[:, 8:16], scalar=1.0, in1=gcol[:], op0=ADD, op1=MULT)
         for g in range(4):
             cond_cast(nc.vector.tensor_copy, 1, g)
-        beta = film(0, 1)
-        g_banks = [gain_to_psum(0, n) for n in range(2)]
         for n in range(2):
-            make_shift(0, n, beta[n])
+            nc.scalar.copy(out=pb[:, cols(n)], in_=pbb[n][:])
         square(0)
         square(1)
-        xb = {0: add_bias(0)}
+        gamma = [film_gamma(0, n) for n in range(2)]
+        fbk = [spread(0, "t", 2), spread(1, "t", 2)]
+        for n in range(2):
+            gain_rows(0, n, gamma[n])
+        cond_banks = [cond_turn(1, g, "y", 4) for g in range(4)]
+        g_banks = [gain_turn(0, 0)]
+        for n in range(2):
+            nc.scalar.copy(out=t_major(fbb[:, cols(n)]), in_=by_t(fbk[n][:]))
         inv_root(0)
-        u = {0: modulate(0, g_banks)}
+        xb = {i: add_bias(i) for i in (0, 1)}
+        xd = {i: deinterleave(nc.vector.tensor_copy, i) for i in (0, 1)}
+        for g in range(4):
+            cond_scale_quant(1, g, cond_banks[g])
+        beta = film_beta(0)
+        g_banks.append(gain_turn(0, 1))
+        u = {0: modulate(0, xd[0], g_banks)}
+        for n in range(2):
+            make_shift(0, n, beta[n])
         square(2)
         square(3)
         inv_root(2)
-        xb[1] = add_bias(1)
-        u[1] = modulate(1, g_banks)
+        for i in (2, 3):
+            xd[i] = deinterleave(nc.scalar.copy, i)
+        u[1] = modulate(1, xd[1], g_banks)
+        gamma = [film_gamma(1, n) for n in range(2)]
+        for n in range(2):
+            gain_rows(1, n, gamma[n])
 
-        cond_banks = {}
         hqs = {}
         codes = {}
         y = {}
         g_next = []
         for s in range(TILES + 3):
+            if s < TILES:
+                hqs[s] = ring.tile([128, 2, 128, 4], BF16, name="hq", tag="hq", bufs=3, align_bytes=64)
             if s + 4 < TILES:
                 square(s + 4)
                 if s % 2 == 1:
                     inv_root(s + 3)
-            if s < TILES:
-                hqs[s] = ring.tile([128, 2, 128, 4], BF16, name="hq", tag="hq", bufs=3, align_bytes=64)
             for n in range(2):
                 if s < TILES:
                     relu(hqs[s], n, turn(s, n, u[s]))
-                if s == 0:
-                    for g in (2 * n, 2 * n + 1):
-                        cond_banks[g] = cond_turn(1, g, "y", 4)
                 if s == 6:
-                    g_next.append(gain_to_psum(1, n))
+                    g_next.append(gain_turn(1, n))
                 if 2 <= s < TILES + 2:
                     y[s - 2, n] = project(codes[s - 2], n)
-            if s == 1:
-                gamma = film(1, 0)
-                beta = film(1, 1)
+            if s == 0:
+                beta = film_beta(1)
+            if s + 4 in ON_SCALAR:
+                xd[s + 4] = deinterleave(nc.scalar.copy, s + 4)
             if s == 6:
                 g_banks = g_next
             if s >= 3:
@@ -316,13 +355,10 @@ def tile_film_modulated_projection_f7_kernel(
             if 1 <= s <= TILES:
                 codes[s - 1] = quant(hqs.pop(s - 1))
             if s + 2 < TILES:
-                u[s + 2] = modulate(s + 2, g_banks)
+                u[s + 2] = modulate(s + 2, xd[s + 2], g_banks)
+            if s + 4 < TILES and s + 4 not in ON_SCALAR:
+                xd[s + 4] = deinterleave(nc.vector.tensor_copy, s + 4)
             if s == 0:
-                for g in range(4):
-                    cond_scale_quant(1, g, cond_banks.pop(g))
-            if s == 1:
-                for n in range(2):
-                    make_gain(1, n, gamma[n])
                 for n in range(2):
                     make_shift(1, n, beta[n])
             if 2 <= s + 1 < TILES:

@@ -21,7 +21,8 @@ ACT = mybir.ActivationFunctionType
 
 N = 512
 TILES = 2 * P
-ON_SCALAR = (6, 8, 10, 12, 14)
+ON_VECTOR = (0, 4, 5, 6, 12)
+ON_GPSIMD = (2, 4, 5, 7, 9, 11, 12, 14)
 
 
 def tile_film_modulated_projection_f7_kernel(
@@ -68,9 +69,9 @@ def tile_film_modulated_projection_f7_kernel(
         msq = const("msq", [128, TILES], F32)
         rstd = const("rstd", [128, TILES], F32)
 
+        nc.gpsimd.memset(sc[:], 0.0)
         nc.gpsimd.memset(neg_half[:], -0.5)
         make_identity(nc, ident[:])
-        nc.vector.memset(sc[:], 0.0)
         nc.vector.memset(vt[:], 0.0)
         nc.vector.memset(vec[:], 0.0)
         nc.vector.memset(fs[:].rearrange("p g n -> p (g n)").bitcast(I32), 0)
@@ -79,7 +80,7 @@ def tile_film_modulated_projection_f7_kernel(
         nc.vector.memset(ps[:].rearrange("p g n -> p (g n)").bitcast(I32), 0)
 
         nc.sync.dma_start(out=cb[0][:], in_=cond_bytes[0:128, :])
-        nc.scalar.dma_start(out=sc[0:4, :], in_=cond_scale.rearrange("o (g n) -> (o g) n", n=N))
+        nc.sync.dma_start(out=sc[0:4, :], in_=cond_scale.rearrange("o (g n) -> (o g) n", n=N))
         nc.scalar.dma_start(out=vt[0:8, :], in_=gain.rearrange("(c m) -> c m", m=128))
         nc.scalar.dma_start(out=vt[8:16, :], in_=film_bias[0:F].rearrange("(c m) -> c m", m=128))
         nc.scalar.dma_start(out=vec[0:2, :], in_=film_bias[F : 2 * F].rearrange("(c n) -> c n", n=N))
@@ -208,14 +209,15 @@ def tile_film_modulated_projection_f7_kernel(
             nc.gpsimd.tensor_tensor(out=rstd[:, c], in0=msq[:, c], in1=neg_half[:], op=POW)
 
         def add_bias(i):
-            pair = []
-            for n in range(2):
-                t = ring.tile([128, N], F32, name="xb%d" % n, tag="xb%d" % n, bufs=4, align_bytes=64)
-                nc.gpsimd.tensor_tensor(out=t[:], in0=xs[:, i, cols(n)], in1=pb[:, cols(n)], op=ADD)
-                pair.append(t)
-            return pair
+            t = ring.tile([128, F], F32, name="xb", tag="xb", bufs=7, align_bytes=64)
+            engine, width = (nc.gpsimd, 256) if i in ON_GPSIMD else (nc.vector, N)
+            for k in range(0, F, width):
+                c = slice(k, k + width)
+                engine.tensor_tensor(out=t[:, c], in0=xs[:, i, c], in1=pb[:, c], op=ADD)
+            return t
 
-        def deinterleave(copy, i):
+        def deinterleave(i):
+            copy = nc.vector.tensor_copy if i in ON_VECTOR else nc.scalar.copy
             t = ring.tile([128, F], BF16, name="xd", tag="xd", bufs=4, align_bytes=64)
             copy(out=t[:].rearrange("q (t c i) -> q c t i", t=4, i=8), in_=xs[:, i, :].rearrange("q (c i t) -> q c t i", t=4, i=8))
             return t
@@ -270,7 +272,7 @@ def tile_film_modulated_projection_f7_kernel(
             o = outs[i]
             h, j = divmod(i, P)
             dst = out[128 * h : 128 * h + 128, j, :]
-            nc.vector.tensor_tensor(out=o[:, cols(n)], in0=b[:], in1=xb[n][:], op=ADD)
+            nc.vector.tensor_tensor(out=o[:, cols(n)], in0=b[:], in1=xb[:, cols(n)], op=ADD)
             if i == TILES - 1:
                 nc.sync.dma_start(out=dst[:, cols(n)], in_=o[:, cols(n)])
             elif n == 1:
@@ -307,7 +309,7 @@ def tile_film_modulated_projection_f7_kernel(
             nc.scalar.copy(out=t_major(fbb[:, cols(n)]), in_=by_t(fbk[n][:]))
         inv_root(0)
         xb = {i: add_bias(i) for i in (0, 1)}
-        xd = {i: deinterleave(nc.vector.tensor_copy, i) for i in (0, 1)}
+        xd = {i: deinterleave(i) for i in (0, 1)}
         for g in range(4):
             cond_scale_quant(1, g, cond_banks[g])
         beta = film_beta(0)
@@ -319,7 +321,7 @@ def tile_film_modulated_projection_f7_kernel(
         square(3)
         inv_root(2)
         for i in (2, 3):
-            xd[i] = deinterleave(nc.scalar.copy, i)
+            xd[i] = deinterleave(i)
         u[1] = modulate(1, xd[1], g_banks)
         gamma = [film_gamma(1, n) for n in range(2)]
         for n in range(2):
@@ -341,25 +343,26 @@ def tile_film_modulated_projection_f7_kernel(
                     relu(hqs[s], n, turn(s, n, u[s]))
                 if s == 6:
                     g_next.append(gain_turn(1, n))
+            for n in range(2):
                 if 2 <= s < TILES + 2:
                     y[s - 2, n] = project(codes[s - 2], n)
             if s == 0:
                 beta = film_beta(1)
-            if s + 4 in ON_SCALAR:
-                xd[s + 4] = deinterleave(nc.scalar.copy, s + 4)
+            if s + 4 < TILES and s + 4 not in ON_VECTOR:
+                xd[s + 4] = deinterleave(s + 4)
             if s == 6:
                 g_banks = g_next
+            if 1 <= s <= TILES:
+                codes[s - 1] = quant(hqs.pop(s - 1))
             if s >= 3:
                 for n in range(2):
                     finish(s - 3, n, y.pop((s - 3, n)), xb[s - 3])
-            if 1 <= s <= TILES:
-                codes[s - 1] = quant(hqs.pop(s - 1))
             if s + 2 < TILES:
                 u[s + 2] = modulate(s + 2, xd[s + 2], g_banks)
-            if s + 4 < TILES and s + 4 not in ON_SCALAR:
-                xd[s + 4] = deinterleave(nc.vector.tensor_copy, s + 4)
+            if s + 4 < TILES and s + 4 in ON_VECTOR:
+                xd[s + 4] = deinterleave(s + 4)
             if s == 0:
                 for n in range(2):
                     make_shift(1, n, beta[n])
-            if 2 <= s + 1 < TILES:
-                xb[s + 1] = add_bias(s + 1)
+            if s + 2 < TILES:
+                xb[s + 2] = add_bias(s + 2)

from contextlib import ExitStack

import concourse.mybir as mybir
from concourse.masks import make_identity

S, P, D, F = 256, 8, 2048, 1024
FLOPS = 2 * S * D * 2 * F + 2 * S * P * F * F

F32 = mybir.dt.float32
BF16 = mybir.dt.bfloat16
I32 = mybir.dt.int32
U32 = mybir.dt.uint32
U8 = mybir.dt.uint8
FP8 = mybir.dt.float8_e4m3fn
FP8X4 = mybir.dt.float8_e4m3fn_x4
FP4X4 = mybir.dt.float4_e2m1fn_x4
ADD = mybir.AluOpType.add
MULT = mybir.AluOpType.mult
POW = mybir.AluOpType.pow
ACT = mybir.ActivationFunctionType

N = 512
TILES = 2 * P
ON_VECTOR = (0, 4, 5, 6, 12)
ON_GPSIMD = (2, 4, 5, 7, 9, 11, 12, 14)


def tile_film_modulated_projection_f7_kernel(
    tc, cond_bytes, cond_scale, film_words, film_scales, film_bias, x, gain,
    proj_words, proj_scales, proj_bias, out,
):
    nc = tc.nc
    with ExitStack() as ctx:
        keep = ctx.enter_context(tc.tile_pool(name="keep", bufs=1))
        ring = ctx.enter_context(tc.tile_pool(name="ring", bufs=3))
        psum = ctx.enter_context(tc.psum_pool(name="psum", bufs=2))
        ctx.enter_context(tc.manual_schedule())

        def const(name, shape, dtype):
            return keep.tile(shape, dtype, name=name, tag=name, align_bytes=64)

        def bank(tag, bufs):
            return psum.tile([128, N], F32, name="bank_" + tag, tag=tag, bufs=bufs)

        ident = const("ident", [128, 128], F32)
        ident_b = const("ident_b", [128, 128], BF16)
        neg_half = const("neg_half", [128, 2], F32)
        turn_fwd = const("turn_fwd", [128, 128], F32)
        sc = const("sc", [128, N], F32)
        vt = const("vt", [128, 128], BF16)
        vec = const("vec", [128, N], BF16)
        gcol = const("gcol", [128, 8], F32)
        g1col = const("g1col", [128, 8], F32)
        csc = const("csc", [128, 4, 4], F32)
        cb = [const("cond_raw%d" % h, [128, D], U8) for h in range(2)]
        cw = [const("cond_wide%d" % h, [128, D], BF16) for h in range(2)]
        cc = [const("cond_codes%d" % h, [128, 4 * 128], U32) for h in range(2)]
        cs = [const("cond_planes%d" % h, [128, 4 * 128], U8) for h in range(2)]
        w1 = const("w1", [128, 8, 2048], U8)
        fs = const("fs", [128, 4, 2048], U8)
        w2 = const("w2", [128, 2, F], U32)
        ps = const("ps", [128, 2, F], U8)
        xs = const("xs", [128, TILES, F], BF16)
        fbb = const("fbb", [128, F], F32)
        pb = const("pb", [128, F], F32)
        gts = [const("gts%d" % h, [128, F], F32) for h in range(2)]
        bsb = [const("bsb%d" % h, [128, F], F32) for h in range(2)]
        ssq = const("ssq", [128, TILES], F32)
        msq = const("msq", [128, TILES], F32)
        rstd = const("rstd", [128, TILES], F32)

        nc.gpsimd.memset(sc[:], 0.0)
        nc.gpsimd.memset(neg_half[:], -0.5)
        make_identity(nc, ident[:])
        nc.vector.memset(vt[:], 0.0)
        nc.vector.memset(vec[:], 0.0)
        nc.vector.memset(fs[:].rearrange("p g n -> p (g n)").bitcast(I32), 0)
        nc.vector.tensor_copy(out=ident_b[:], in_=ident[:])
        nc.vector.tensor_copy(out=turn_fwd[:].rearrange("q (t p) -> q t p", t=4), in_=ident[:].rearrange("q (p t) -> q t p", t=4))
        nc.vector.memset(ps[:].rearrange("p g n -> p (g n)").bitcast(I32), 0)

        nc.sync.dma_start(out=cb[0][:], in_=cond_bytes[0:128, :])
        nc.sync.dma_start(out=sc[0:4, :], in_=cond_scale.rearrange("o (g n) -> (o g) n", n=N))
        nc.scalar.dma_start(out=vt[0:8, :], in_=gain.rearrange("(c m) -> c m", m=128))
        nc.scalar.dma_start(out=vt[8:16, :], in_=film_bias[0:F].rearrange("(c m) -> c m", m=128))
        nc.scalar.dma_start(out=vec[0:2, :], in_=film_bias[F : 2 * F].rearrange("(c n) -> c n", n=N))
        nc.scalar.dma_start(out=vec[2:4, :], in_=proj_bias.rearrange("(c n) -> c n", n=N))
        nc.scalar.activation(out=rstd[:, 0:1], in_=neg_half[:, 0:1], func=ACT.Square)
        fsi = fs[:].bitcast(I32)
        fsd = film_scales.bitcast(I32)
        w1i = w1[:].bitcast(I32)
        w1d = film_words.bitcast(I32)

        def load_w1(half):
            for g in range(4):
                nc.sync.dma_start(out=w1i[:, 4 * half + g, :], in_=w1d[g, :, 512 * half : 512 * half + 512])

        def load_x(pair):
            half, j = divmod(2 * pair, P)
            nc.sync.dma_start(out=xs[:, 2 * pair : 2 * pair + 2, :], in_=x[128 * half : 128 * half + 128, j : j + 2, :])

        load_w1(0)
        for q in range(4):
            nc.sync.dma_start(out=fsi[32 * q : 32 * q + 4, :, :], in_=fsd[:, 4 * q : 4 * q + 4, :].rearrange("g q n -> q g n"))
        load_x(0)
        nc.sync.dma_start(out=cb[1][:], in_=cond_bytes[128:256, :])
        load_w1(1)
        load_x(1)
        psi = ps[:].bitcast(I32)
        psd = proj_scales.bitcast(I32)
        for q in range(4):
            nc.sync.dma_start(out=psi[32 * q : 32 * q + 4, :, :], in_=psd[:, 4 * q : 4 * q + 4, :].rearrange("g q n -> q g n"))
        w2d = proj_words.rearrange("g p n t -> g p (n t)").bitcast(I32)
        for g in range(2):
            nc.sync.dma_start(out=w2[:, g, :].bitcast(I32), in_=w2d[g])
        for pair in range(2, 8):
            load_x(pair)

        def spread(c, tag, bufs):
            b = bank(tag, bufs)
            nc.tensor.matmul(b[:], lhsT=ident_b[:, c : c + 1].to_broadcast([128, 128]), rhs=vec[:], start=True, stop=True)
            return b

        def by_t(ap):
            return ap.rearrange("q (p t) -> q t p", t=4)

        def t_major(ap):
            return ap.rearrange("q (t p) -> q t p", t=4)

        def cols(n):
            return slice(N * n, N * n + N)

        def cond_cast(copy, h, g):
            copy(out=cw[h][:, cols(g)], in_=cb[h][:, cols(g)].bitcast(FP8))

        def cond_turn(h, g, tag, bufs):
            words = cw[h][:].bitcast(F32)
            b = bank(tag, bufs)
            for u in range(2):
                nc.tensor.transpose(b[:, 128 * u : 128 * u + 128], words[:, 256 * g + u : 256 * g + 256 : 2], ident[:])
            return b

        def cond_scale_quant(h, g, b):
            t = ring.tile([128, 128, 4], BF16, name="cq", tag="cq", bufs=2, align_bytes=64)
            src = b[:, 0:256].bitcast(BF16).rearrange("p (u s e) -> p s u e", u=2, e=2)
            dst = t[:].rearrange("p s (u e) -> p s u e", u=2)
            sc = csc[:, g, :].rearrange("p (u e) -> p u e", u=2).unsqueeze(1).to_broadcast([128, 128, 2, 2])
            nc.vector.tensor_tensor(out=dst, in0=src, in1=sc, op=MULT)
            nc.vector.quantize_mx(
                out=cc[h][:, 128 * g : 128 * g + 128].bitcast(FP8X4),
                scales=cs[h][:, 128 * g : 128 * g + 128],
                in_=t[:].rearrange("p s t -> p (s t)"),
            )

        def film_beta(h):
            banks = [bank("y", 4), bank("y", 4)]
            for g in range(4):
                for n in range(2):
                    nc.tensor.matmul_mx(
                        out=banks[n][:],
                        lhsT=cc[h][:, 128 * g : 128 * g + 128].bitcast(FP8X4),
                        lhsT_scale=cs[h][:, 128 * g : 128 * g + 128],
                        rhs=w1[:, 4 + g, 1024 * n : 1024 * n + 1024].bitcast(FP4X4),
                        rhs_scale=fs[:, g, F + N * n : F + N * n + N],
                        start=(g == 0),
                        stop=(g == 3),
                    )
            return banks

        def film_gamma(h, n):
            b = bank("y", 4)
            for c in range(4 * n, 4 * n + 4):
                for g in range(4):
                    nc.tensor.matmul_mx(
                        out=b[:, 128 * (c % 4) : 128 * (c % 4) + 128],
                        lhsT=w1[:, g, 256 * c : 256 * c + 256].bitcast(FP4X4),
                        lhsT_scale=fs[:, g, 128 * c : 128 * c + 128],
                        rhs=cc[h][:, 128 * g : 128 * g + 128].bitcast(FP8X4),
                        rhs_scale=cs[h][:, 128 * g : 128 * g + 128],
                        start=(g == 0),
                        stop=(g == 3),
                    )
            return b

        def gain_rows(h, n, b):
            for c in range(4 * n, 4 * n + 4):
                nc.scalar.activation(
                    out=gts[h][:, 128 * c : 128 * c + 128], in_=b[:, 128 * (c % 4) : 128 * (c % 4) + 128],
                    func=ACT.Identity, scale=gcol[:, c : c + 1], bias=g1col[:, c : c + 1],
                )

        def gain_turn(h, n):
            b = bank("g", 2)
            for c in range(4):
                k = N * n + 128 * c
                nc.tensor.transpose(t_major(b[:])[:, :, 32 * c : 32 * c + 32], gts[h][:, k : k + 128], turn_fwd[:])
            return b

        def make_shift(h, n, b):
            nc.vector.tensor_tensor(out=t_major(bsb[h][:, cols(n)]), in0=by_t(b[:]), in1=t_major(fbb[:, cols(n)]), op=ADD)

        def square(i):
            junk = ring.tile([128, F], BF16, name="junk", tag="junk", bufs=2, align_bytes=64)
            nc.scalar.activation(out=junk[:], in_=xs[:, i, :], func=ACT.Square, accum_out=ssq[:, i : i + 1])

        def inv_root(i):
            c = slice(i, i + 2)
            nc.gpsimd.tensor_scalar(msq[:, c], ssq[:, c], 1.0 / F, 0.1, MULT, ADD)
            nc.gpsimd.tensor_tensor(out=rstd[:, c], in0=msq[:, c], in1=neg_half[:], op=POW)

        def add_bias(i):
            t = ring.tile([128, F], F32, name="xb", tag="xb", bufs=7, align_bytes=64)
            engine, width = (nc.gpsimd, 256) if i in ON_GPSIMD else (nc.vector, N)
            for k in range(0, F, width):
                c = slice(k, k + width)
                engine.tensor_tensor(out=t[:, c], in0=xs[:, i, c], in1=pb[:, c], op=ADD)
            return t

        def deinterleave(i):
            copy = nc.vector.tensor_copy if i in ON_VECTOR else nc.scalar.copy
            t = ring.tile([128, F], BF16, name="xd", tag="xd", bufs=4, align_bytes=64)
            copy(out=t[:].rearrange("q (t c i) -> q c t i", t=4, i=8), in_=xs[:, i, :].rearrange("q (c i t) -> q c t i", t=4, i=8))
            return t

        def modulate(i, xd, g_banks):
            u = ring.tile([128, F], F32, name="u", tag="u", bufs=4, align_bytes=64)
            for n in range(2):
                nc.vector.scalar_tensor_tensor(
                    out=t_major(u[:, cols(n)]), in0=xd[:].rearrange("q (t g p) -> q g t p", t=4, g=2)[:, n, :, :], scalar=rstd[:, i : i + 1],
                    in1=t_major(g_banks[n][:]), op0=MULT, op1=MULT,
                )
            return u

        def turn(i, n, u):
            b = bank("t", 2)
            for t in range(4):
                o = b[:, 128 * t : 128 * t + 128]
                c = slice(N * n + 128 * t, N * n + 128 * t + 128)
                nc.tensor.matmul(o, lhsT=u[:, c], rhs=ident[:], start=True, stop=False, is_transpose=True)
                nc.tensor.matmul(o, lhsT=bsb[i // P][:, c], rhs=ident[:], start=False, stop=True, is_transpose=True)
            return b

        def relu(hq, n, b):
            nc.scalar.activation(out=hq[:, n, :, :], in_=b[:].rearrange("p (t s) -> p s t", t=4), func=ACT.Relu)

        def quant(hq):
            hc = ring.tile([128, 256], U32, name="hc", tag="hc", bufs=3, align_bytes=64)
            hs = ring.tile([128, 256], U8, name="hs", tag="hs", bufs=3, align_bytes=64)
            nc.vector.quantize_mx(out=hc[:].bitcast(FP8X4), scales=hs[:], in_=hq[:].rearrange("p g s t -> p (g s t)"))
            return hc, hs

        def project(codes, n):
            hc, hs = codes
            b = bank("y", 4)
            for g in range(2):
                nc.tensor.matmul_mx(
                    out=b[:],
                    lhsT=hc[:, 128 * g : 128 * g + 128].bitcast(FP8X4),
                    lhsT_scale=hs[:, 128 * g : 128 * g + 128],
                    rhs=w2[:, g, cols(n)].bitcast(FP8X4),
                    rhs_scale=ps[:, g, cols(n)],
                    start=(g == 0),
                    stop=(g == 1),
                )
            return b

        outs = {}

        def finish(i, n, b, xb):
            if n == 0:
                outs[i] = ring.tile([128, F], F32, name="o", tag="o", bufs=4, align_bytes=64)
            o = outs[i]
            h, j = divmod(i, P)
            dst = out[128 * h : 128 * h + 128, j, :]
            nc.vector.tensor_tensor(out=o[:, cols(n)], in0=b[:], in1=xb[:, cols(n)], op=ADD)
            if i == TILES - 1:
                nc.sync.dma_start(out=dst[:, cols(n)], in_=o[:, cols(n)])
            elif n == 1:
                nc.sync.dma_start(out=dst, in_=o[:])

        tb = bank("t", 2)
        for t in range(4):
            nc.tensor.transpose(tb[:, 128 * t : 128 * t + 128], sc[:, t::4], ident[:])
        nc.vector.tensor_copy(out=csc[:], in_=tb[:].rearrange("p (t r) -> p r t", t=4)[:, 0:4, :])
        for g in range(4):
            cond_cast((nc.scalar.copy, nc.vector.tensor_copy)[g % 2], 0, g)
        for g in range(4):
            b = cond_turn(0, g, "t", 2)
            cond_scale_quant(0, g, b)
            if g == 1:
                pbb = [spread(2, "y", 4), spread(3, "y", 4)]
                vb = psum.tile([128, 2 * N], BF16, name="bank_v", tag="g", bufs=2)
                nc.tensor.transpose(vb[:, 0:128], vt[:], ident_b[:])
        nc.vector.tensor_copy(out=gcol[:], in_=vb[:, 0:8])
        nc.vector.scalar_tensor_tensor(out=g1col[:], in0=vb[:, 8:16], scalar=1.0, in1=gcol[:], op0=ADD, op1=MULT)
        for g in range(4):
            cond_cast(nc.vector.tensor_copy, 1, g)
        for n in range(2):
            nc.scalar.copy(out=pb[:, cols(n)], in_=pbb[n][:])
        square(0)
        square(1)
        gamma = [film_gamma(0, n) for n in range(2)]
        fbk = [spread(0, "t", 2), spread(1, "t", 2)]
        for n in range(2):
            gain_rows(0, n, gamma[n])
        cond_banks = [cond_turn(1, g, "y", 4) for g in range(4)]
        g_banks = [gain_turn(0, 0)]
        for n in range(2):
            nc.scalar.copy(out=t_major(fbb[:, cols(n)]), in_=by_t(fbk[n][:]))
        inv_root(0)
        xb = {i: add_bias(i) for i in (0, 1)}
        xd = {i: deinterleave(i) for i in (0, 1)}
        for g in range(4):
            cond_scale_quant(1, g, cond_banks[g])
        beta = film_beta(0)
        g_banks.append(gain_turn(0, 1))
        u = {0: modulate(0, xd[0], g_banks)}
        for n in range(2):
            make_shift(0, n, beta[n])
        square(2)
        square(3)
        inv_root(2)
        for i in (2, 3):
            xd[i] = deinterleave(i)
        u[1] = modulate(1, xd[1], g_banks)
        gamma = [film_gamma(1, n) for n in range(2)]
        for n in range(2):
            gain_rows(1, n, gamma[n])

        hqs = {}
        codes = {}
        y = {}
        g_next = []
        for s in range(TILES + 3):
            if s < TILES:
                hqs[s] = ring.tile([128, 2, 128, 4], BF16, name="hq", tag="hq", bufs=3, align_bytes=64)
            if s + 4 < TILES:
                square(s + 4)
                if s % 2 == 1:
                    inv_root(s + 3)
            for n in range(2):
                if s < TILES:
                    relu(hqs[s], n, turn(s, n, u[s]))
                if s == 6:
                    g_next.append(gain_turn(1, n))
            for n in range(2):
                if 2 <= s < TILES + 2:
                    y[s - 2, n] = project(codes[s - 2], n)
            if s == 0:
                beta = film_beta(1)
            if s + 4 < TILES and s + 4 not in ON_VECTOR:
                xd[s + 4] = deinterleave(s + 4)
            if s == 6:
                g_banks = g_next
            if 1 <= s <= TILES:
                codes[s - 1] = quant(hqs.pop(s - 1))
            if s >= 3:
                for n in range(2):
                    finish(s - 3, n, y.pop((s - 3, n)), xb[s - 3])
            if s + 2 < TILES:
                u[s + 2] = modulate(s + 2, xd[s + 2], g_banks)
            if s + 4 < TILES and s + 4 in ON_VECTOR:
                xd[s + 4] = deinterleave(s + 4)
            if s == 0:
                for n in range(2):
                    make_shift(1, n, beta[n])
            if s + 2 < TILES:
                xb[s + 2] = add_bias(s + 2)
